import numpy as np
import ml_dtypes


def mxq(x, axis, fmt="e4m3"):
    dtype, down = {"e4m3": (ml_dtypes.float8_e4m3fn, 7), "e5m2": (ml_dtypes.float8_e5m2, 14)}[fmt]
    v = np.moveaxis(np.asarray(x, np.float32).astype(ml_dtypes.bfloat16).astype(np.float64), axis, -1)
    blocks = v.reshape(v.shape[:-1] + (-1, 32))
    amax = np.abs(blocks).max(-1, keepdims=True)
    byte = np.maximum(np.where(amax > 0, np.frexp(amax)[1] - 1 + 127, 0) - down, 1)
    scale = np.exp2(byte - 127.0)
    codes = (blocks / scale).astype(np.float32).astype(dtype).astype(np.float64)
    return np.moveaxis((codes * scale).reshape(v.shape), -1, axis)


WIDE = False


def mx_kscale(k):
    if not WIDE:
        return np.ones(k)
    levels = np.array([30, -30])
    if k % 512:
        return np.exp2(np.random.permutation(np.resize(levels, k // 32))).repeat(32)
    a = np.empty((k // 512, 16))
    for p in range(k // 512):
        a[p, :8] = np.random.permutation(np.resize(levels, 8))
        for g in range(8):
            far = levels[np.abs(levels - a[p, g]) >= 10]
            a[p, g + 8] = far[np.random.randint(len(far))]
    return np.exp2(a.ravel()).repeat(32)


def f64(x):
    return np.asarray(x).astype(np.float64)


def striped(idx):
    return np.tile(np.asarray(idx).reshape(-1, 16).T, (8, 1)).astype(np.uint16)


def unstriped(offs):
    return offs[:16].T.reshape(-1).astype(np.int64)


E2M1 = np.array([0.0, 0.5, 1.0, 1.5, 2.0, 3.0, 4.0, 6.0, -0.0, -0.5, -1.0, -1.5, -2.0, -3.0, -4.0, -6.0])


def pack_weight(w, fmt):
    k, n = w.shape
    w = f64(np.asarray(w, np.float32).astype(ml_dtypes.bfloat16)).reshape(k // 32, 32, n)
    amax = np.abs(w).max(1)
    if fmt in ("e4m3", "e5m2"):
        byte = np.frexp(amax)[1] - 1 + 127 - (7 if fmt == "e4m3" else 14)
    else:
        mant, ex = np.frexp(amax / 6.0)
        byte = np.where(mant > 0.5, ex, ex - 1) + 127
    byte = np.clip(np.where(amax > 0, byte, 1), 1, 254)
    scaled = (w * np.exp2(127.0 - byte)[:, None, :]).reshape(k, n).astype(np.float32)
    by_word = np.ascontiguousarray(scaled.reshape(k // 512, 128, 4, n).transpose(0, 1, 3, 2))
    if fmt in ("e4m3", "e5m2"):
        words = by_word.astype(ml_dtypes.float8_e4m3fn if fmt == "e4m3" else ml_dtypes.float8_e5m2).view(np.uint8)
    else:
        c = by_word.astype(ml_dtypes.float4_e2m1fn).view(np.uint8) & 0xF
        words = (c[..., 0::2] | (c[..., 1::2] << 4)).reshape(k // 512, 128, 2 * n)
    return np.ascontiguousarray(words), np.ascontiguousarray(byte.astype(np.uint8).reshape(k // 512, 16, n))


def unpack_weight(words, scales, fmt):
    g, _, n = scales.shape
    words = np.ascontiguousarray(words).reshape(g, 128, n, -1)
    if fmt in ("e4m3", "e5m2"):
        vals = words.view(ml_dtypes.float8_e4m3fn if fmt == "e4m3" else ml_dtypes.float8_e5m2).astype(np.float64)
    else:
        nib = np.empty((g, 128, n, 4), np.uint8)
        nib[..., 0::2] = words & 0xF
        nib[..., 1::2] = words >> 4
        vals = E2M1[nib]
    vals = vals * np.repeat(np.exp2(scales.astype(np.float64) - 127.0), 8, axis=1)[..., None]
    return vals.transpose(0, 1, 3, 2).reshape(g * 512, n)


def e4m3fn_bytes(y):
    return np.clip(np.asarray(y, np.float64), -448.0, 448.0).astype(np.float32).astype(ml_dtypes.float8_e4m3fn).view(np.uint8)


def e4m3fn_values(b):
    return np.asarray(b, np.uint8).view(ml_dtypes.float8_e4m3fn).astype(np.float64)


K, V, D, J, N = 512, 512, 512, 256, 256


def setup_inputs():
    n = np.random.standard_normal
    idx = np.random.permutation(V)[:J]
    idx2 = np.random.permutation(D)[:J]
    fk = mx_kscale(K)
    wp = pack_weight(n((K, N)) * 1 / np.sqrt(K) / fk[:, None], "e5m2")
    w2p = pack_weight(n((K, N)) * 1 / np.sqrt(K) / fk[:, None], "e4m3")
    return {
        "ca": e4m3fn_bytes(np.random.randint(-15, 16, (K, V)).astype(np.float64)),
        "cb": e4m3fn_bytes(np.random.randint(-15, 16, (K, V)).astype(np.float64)),
        "cd": e4m3fn_bytes(np.random.randint(-15, 16, (K, D)).astype(np.float64)),
        "ce": e4m3fn_bytes(np.random.randint(-15, 16, (K, D)).astype(np.float64)),
        "sa": (np.random.uniform(0.005, 0.015, (K, 1)) * fk[:, None]).astype(np.float32),
        "sb": (np.random.uniform(0.005, 0.015, (K, 1)) * fk[:, None]).astype(np.float32),
        "w_words": wp[0],
        "w_scales": wp[1],
        "w2_words": w2p[0],
        "w2_scales": w2p[1],
        "offs": striped(idx),
        "offs2": striped(idx2),
    }


def reference(ca, cb, cd, ce, sa, sb, w_words, w_scales, w2_words, w2_scales, offs, offs2):
    idx = unstriped(offs)
    idx2 = unstriped(offs2)
    wu = unpack_weight(w_words, w_scales, "e5m2")
    w2u = unpack_weight(w2_words, w2_scales, "e4m3")
    z1 = (e4m3fn_values(ca)[:, idx] * e4m3fn_values(cd)[:, idx2] - e4m3fn_values(cb)[:, idx] * e4m3fn_values(ce)[:, idx2]) * f64(sa)
    z2 = (e4m3fn_values(ca)[:, idx] * e4m3fn_values(ce)[:, idx2] + e4m3fn_values(cb)[:, idx] * e4m3fn_values(cd)[:, idx2]) * f64(sb)
    z1q = mxq(z1, 0, "e4m3")
    z2q = mxq(z2, 0, "e4m3")
    p = wu.T @ z1q + w2u.T @ z2q
    return p

@@ -1,0 +1,135 @@
+from contextlib import ExitStack
+
+import concourse.mybir as mybir
+
+K, V, J, N = 512, 512, 256, 256
+FLOPS = 2 * 2 * K * N * J
+
+F32 = mybir.dt.float32
+BF16 = mybir.dt.bfloat16
+I32 = mybir.dt.int32
+U32 = mybir.dt.uint32
+U16 = mybir.dt.uint16
+U8 = mybir.dt.uint8
+FP8 = mybir.dt.float8_e4m3fn
+E4M3X4 = mybir.dt.float8_e4m3fn_x4
+E5M2X4 = mybir.dt.float8_e5m2_x4
+MULT = mybir.AluOpType.mult
+ADD = mybir.AluOpType.add
+SUB = mybir.AluOpType.subtract
+COPY = mybir.ActivationFunctionType.Copy
+
+P = 128
+PACK = 4
+
+
+def tile_list_turnedpairs_kernel(tc, ca, cb, cd, ce, sa, sb, w_words, w_scales, w2_words, w2_scales, offs, offs2, out):
+    nc = tc.nc
+    with ExitStack() as ctx:
+        keep = ctx.enter_context(tc.tile_pool(name="keep", bufs=1))
+        psum = ctx.enter_context(tc.psum_pool(name="psum", bufs=1))
+
+        list1 = keep.tile([P, J // 16], U16, name="list1")
+        list2 = keep.tile([P, J // 16], U16, name="list2")
+        nc.sync.dma_start(list2[:], offs2)
+        nc.sync.dma_start(list1[:], offs)
+
+        sources = {"d": (cd, list2), "e": (ce, list2), "a": (ca, list1), "b": (cb, list1)}
+        order = [(x, t) for t in (0, 1) for x in "daeb"] + [(x, t) for x in "deab" for t in (2, 3)]
+        tables = {}
+        steps = {}
+        for x, t in order:
+            tables[x, t] = keep.tile([P, V], U8, name="table_%s%d" % (x, t))
+            nc.sync.dma_start(tables[x, t][:], sources[x][0].rearrange("(p t) v -> t p v", t=PACK)[t])
+            if (x, t) == ("b", 1):
+                for z, src in ((0, sa), (1, sb)):
+                    steps[z] = keep.tile([P, PACK], F32, name="step%d" % z)
+                    nc.sync.dma_start(steps[z][:], src.rearrange("(p t) o -> p (t o)", t=PACK))
+
+        w_codes = {}
+        w_plane = keep.tile([P, 2 * N], U8, name="w_plane", align_bytes=64)
+        nc.gpsimd.memset(w_plane[:].bitcast(U32), 0)
+        for z, words in ((0, w_words), (1, w2_words)):
+            w_codes[z] = keep.tile([P, N], U32, name="w_codes%d" % z, align_bytes=64)
+            nc.sync.dma_start(w_codes[z][:].bitcast(I32), words[0].rearrange("p n r -> p (n r)").bitcast(I32))
+        for z, scales in ((0, w_scales), (1, w2_scales)):
+            for q in range(4):
+                nc.sync.dma_start(
+                    w_plane[32 * q : 32 * q + 4, z * N : (z + 1) * N].bitcast(I32),
+                    scales[0][4 * q : 4 * q + 4, :].bitcast(I32),
+                )
+
+        early = {x: keep.tile([P, 2 * J], U8, name="early_" + x) for x in sources}
+        late = {x: keep.tile([P, (1 if x == "b" else 2) * J], U8, name="late_" + x, tag="late_" + x) for x in sources}
+        wide = {x: keep.tile([P, 2 * J], F32, name="wide_" + x) for x in sources}
+        prod = {xy: keep.tile([P, PACK * J], F32, name="prod_" + xy) for xy in ("ad", "ae", "be", "bd")}
+        late_wide = {y: keep.tile([P, 2 * J], F32, name="late_wide_" + y) for y in "de"}
+        rounded = [keep.tile([P, J * PACK], BF16, name="rounded%d" % z, align_bytes=64) for z in range(2)]
+
+        def cols(t, n=1):
+            return slice(t * J, (t + n) * J)
+
+        def codes(x, t, n=1):
+            if t < 2:
+                return early[x][:, cols(t, n)]
+            return late[x][:, cols(0 if x == "b" else t - 2, n)]
+
+        def gather(x, t):
+            nc.vector.tensor_copy(codes(x, t), tables[x, t][:].indirect(sources[x][1][:]))
+
+        def finish(z, t, whole):
+            nc.scalar.activation(rounded[z][:, t : J * PACK : PACK], whole, COPY, scale=steps[z][:, t : t + 1])
+
+        for t in (0, 1):
+            for x in "daeb":
+                gather(x, t)
+                nc.scalar.activation(wide[x][:, cols(t)], codes(x, t).bitcast(FP8), COPY)
+        for x, t in order[8:-1]:
+            gather(x, t)
+        for t in (0, 1):
+            if t == 0:
+                whole = [late_wide[y][:, cols(0)] for y in "de"]
+            else:
+                whole = [keep.tile([P, J], F32, name="whole_e", tag="late_e")[:], prod["ad"][:, cols(t)]]
+            for xy in ("ad", "ae", "be"):
+                nc.gpsimd.tensor_tensor(prod[xy][:, cols(t)], wide[xy[0]][:, cols(t)], wide[xy[1]][:, cols(t)], MULT)
+            nc.gpsimd.tensor_tensor(whole[0], prod["ad"][:, cols(t)], prod["be"][:, cols(t)], SUB)
+            nc.gpsimd.tensor_tensor(prod["bd"][:, cols(t)], wide["b"][:, cols(t)], wide["d"][:, cols(t)], MULT)
+            nc.gpsimd.tensor_tensor(whole[1], prod["ae"][:, cols(t)], prod["bd"][:, cols(t)], ADD)
+            for z in range(2):
+                finish(z, t, whole[z])
+                if t == 0:
+                    nc.scalar.activation(late_wide["de"[z]][:], codes("de"[z], 2, 2).bitcast(FP8), COPY)
+        for y in "de":
+            nc.vector.tensor_tensor(prod["a" + y][:, cols(2, 2)], codes("a", 2, 2).bitcast(FP8), late_wide[y][:], MULT)
+        for t in (2, 3):
+            whole = keep.tile([P, 2 * J], F32, name="whole%d" % t)
+            for y in "ed":
+                nc.vector.tensor_tensor(prod["b" + y][:, cols(t)], codes("b", t).bitcast(FP8), late_wide[y][:, cols(t - 2)], MULT)
+            nc.vector.tensor_tensor(whole[:, cols(0)], prod["ad"][:, cols(t)], prod["be"][:, cols(t)], SUB)
+            finish(0, t, whole[:, cols(0)])
+            if t == 2:
+                gather("b", 3)
+            nc.vector.tensor_tensor(whole[:, cols(1)], prod["ae"][:, cols(t)], prod["bd"][:, cols(t)], ADD)
+            finish(1, t, whole[:, cols(1)])
+
+        z_codes = [keep.tile([P, J], U32, name="z_codes%d" % z, align_bytes=64) for z in range(2)]
+        z_plane = [keep.tile([P, J], U8, name="z_plane%d" % z, align_bytes=64) for z in range(2)]
+        acc = [psum.tile([P, J], F32, name="acc%d" % m) for m in range(2)]
+        for z, w_dtype in ((0, E5M2X4), (1, E4M3X4)):
+            nc.vector.quantize_mx(out=z_codes[z][:].bitcast(E4M3X4), scales=z_plane[z][:], in_=rounded[z][:])
+            for m in range(2):
+                nc.tensor.matmul_mx(
+                    out=acc[m][:],
+                    lhsT=w_codes[z][:, m * P : (m + 1) * P].bitcast(w_dtype),
+                    lhsT_scale=w_plane[:, z * N + m * P : z * N + (m + 1) * P],
+                    rhs=z_codes[z][:].bitcast(E4M3X4),
+                    rhs_scale=z_plane[z][:],
+                    start=(z == 0),
+                    stop=(z == 1),
+                )
+        result = [keep.tile([P, J], F32, name="result%d" % m) for m in range(2)]
+        nc.scalar.copy(result[0][:], acc[0][:])
+        nc.scalar.dma_start(out[0:P, :], result[0][:])
+        nc.vector.tensor_copy(result[1][:], acc[1][:])
+        nc.sync.dma_start(out[P : 2 * P, :], result[1][:])

@@ -1,6 +1,7 @@
 from contextlib import ExitStack
 
 import concourse.mybir as mybir
+from concourse.masks import make_identity
 
 K, V, J, N = 512, 512, 256, 256
 FLOPS = 2 * 2 * K * N * J
@@ -31,17 +32,19 @@ def tile_list_turnedpairs_kernel(tc, ca, cb, cd, ce, sa, sb, w_words, w_scales, 
 
         list1 = keep.tile([P, J // 16], U16, name="list1")
         list2 = keep.tile([P, J // 16], U16, name="list2")
-        nc.sync.dma_start(list2[:], offs2)
-        nc.sync.dma_start(list1[:], offs)
 
         sources = {"d": (cd, list2), "e": (ce, list2), "a": (ca, list1), "b": (cb, list1)}
-        order = [(x, t) for t in (0, 1) for x in "daeb"] + [(x, t) for x in "deab" for t in (2, 3)]
+        order = [(x, t) for t in range(PACK) for x in "deab"]
         tables = {}
         steps = {}
         for x, t in order:
             tables[x, t] = keep.tile([P, V], U8, name="table_%s%d" % (x, t))
             nc.sync.dma_start(tables[x, t][:], sources[x][0].rearrange("(p t) v -> t p v", t=PACK)[t])
-            if (x, t) == ("b", 1):
+            if (x, t) == ("d", 0):
+                nc.sync.dma_start(list2[:], offs2)
+            if (x, t) == ("e", 0):
+                nc.sync.dma_start(list1[:], offs)
+            if (x, t) == ("b", 0):
                 for z, src in ((0, sa), (1, sb)):
                     steps[z] = keep.tile([P, PACK], F32, name="step%d" % z)
                     nc.sync.dma_start(steps[z][:], src.rearrange("(p t) o -> p (t o)", t=PACK))
@@ -59,77 +62,98 @@ def tile_list_turnedpairs_kernel(tc, ca, cb, cd, ce, sa, sb, w_words, w_scales, 
                     scales[0][4 * q : 4 * q + 4, :].bitcast(I32),
                 )
 
-        early = {x: keep.tile([P, 2 * J], U8, name="early_" + x) for x in sources}
-        late = {x: keep.tile([P, (1 if x == "b" else 2) * J], U8, name="late_" + x, tag="late_" + x) for x in sources}
-        wide = {x: keep.tile([P, 2 * J], F32, name="wide_" + x) for x in sources}
-        prod = {xy: keep.tile([P, PACK * J], F32, name="prod_" + xy) for xy in ("ad", "ae", "be", "bd")}
-        late_wide = {y: keep.tile([P, 2 * J], F32, name="late_wide_" + y) for y in "de"}
+        ident = keep.tile([P, P], F32, name="ident")
+        make_identity(nc, ident[:])
+        picked = {x: keep.tile([P, J], U8, name="picked_" + x) for x in "ab"}
+        wide = {y: keep.tile([P, PACK * J], F32, name="wide_" + y) for y in "den"}
         rounded = [keep.tile([P, J * PACK], BF16, name="rounded%d" % z, align_bytes=64) for z in range(2)]
+        halves = [slice(0, P), slice(P, J)]
 
-        def cols(t, n=1):
-            return slice(t * J, (t + n) * J)
+        def cols(t):
+            return slice(t * J, (t + 1) * J)
 
-        def codes(x, t, n=1):
-            if t < 2:
-                return early[x][:, cols(t, n)]
-            return late[x][:, cols(0 if x == "b" else t - 2, n)]
+        def gather(into, x, t):
+            nc.vector.tensor_copy(into[:], tables[x, t][:].indirect(sources[x][1][:]))
 
-        def gather(x, t):
-            nc.vector.tensor_copy(codes(x, t), tables[x, t][:].indirect(sources[x][1][:]))
+        def gather_and_widen(t):
+            for y in "de":
+                tag = "term_a" + y
+                codes = keep.tile([P, J], U8, name="second", tag=tag)
+                gather(codes, y, t)
+                nc.scalar.activation(wide[y][:, cols(t)], codes[:].bitcast(FP8), COPY)
+                if y == "e" and t < 3:
+                    nc.scalar.activation(wide["n"][:, cols(t)], codes[:].bitcast(FP8), COPY, scale=-1.0)
 
-        def finish(z, t, whole):
-            nc.scalar.activation(rounded[z][:, t : J * PACK : PACK], whole, COPY, scale=steps[z][:, t : t + 1])
+        def finish(z, t, whole, part=slice(0, J)):
+            nc.scalar.activation(rounded[z][:, part.start * PACK + t : part.stop * PACK : PACK], whole, COPY, scale=steps[z][:, t : t + 1])
 
-        for t in (0, 1):
-            for x in "daeb":
-                gather(x, t)
-                nc.scalar.activation(wide[x][:, cols(t)], codes(x, t).bitcast(FP8), COPY)
-        for x, t in order[8:-1]:
-            gather(x, t)
-        for t in (0, 1):
-            if t == 0:
-                whole = [late_wide[y][:, cols(0)] for y in "de"]
-            else:
-                whole = [keep.tile([P, J], F32, name="whole_e", tag="late_e")[:], prod["ad"][:, cols(t)]]
-            for xy in ("ad", "ae", "be"):
-                nc.gpsimd.tensor_tensor(prod[xy][:, cols(t)], wide[xy[0]][:, cols(t)], wide[xy[1]][:, cols(t)], MULT)
-            nc.gpsimd.tensor_tensor(whole[0], prod["ad"][:, cols(t)], prod["be"][:, cols(t)], SUB)
-            nc.gpsimd.tensor_tensor(prod["bd"][:, cols(t)], wide["b"][:, cols(t)], wide["d"][:, cols(t)], MULT)
-            nc.gpsimd.tensor_tensor(whole[1], prod["ae"][:, cols(t)], prod["bd"][:, cols(t)], ADD)
-            for z in range(2):
-                finish(z, t, whole[z])
-                if t == 0:
-                    nc.scalar.activation(late_wide["de"[z]][:], codes("de"[z], 2, 2).bitcast(FP8), COPY)
-        for y in "de":
-            nc.vector.tensor_tensor(prod["a" + y][:, cols(2, 2)], codes("a", 2, 2).bitcast(FP8), late_wide[y][:], MULT)
-        for t in (2, 3):
-            whole = keep.tile([P, 2 * J], F32, name="whole%d" % t)
-            for y in "ed":
-                nc.vector.tensor_tensor(prod["b" + y][:, cols(t)], codes("b", t).bitcast(FP8), late_wide[y][:, cols(t - 2)], MULT)
-            nc.vector.tensor_tensor(whole[:, cols(0)], prod["ad"][:, cols(t)], prod["be"][:, cols(t)], SUB)
-            finish(0, t, whole[:, cols(0)])
-            if t == 2:
-                gather("b", 3)
-            nc.vector.tensor_tensor(whole[:, cols(1)], prod["ae"][:, cols(t)], prod["bd"][:, cols(t)], ADD)
-            finish(1, t, whole[:, cols(1)])
+        gather_and_widen(0)
+        for t in range(PACK):
+            gather(picked["a"], "a", t)
+            gather(picked["b"], "b", t)
+            backs = []
+            for z, pairs in enumerate((("ad", "bn" if t < 3 else "be"), ("ae", "bd"))):
+                terms = []
+                for x, y in pairs:
+                    term = keep.tile([P, J], F32, name="term", tag="term_" + x + y)
+                    nc.vector.tensor_tensor(term[:], picked[x][:].bitcast(FP8), wide[y][:, cols(t)], MULT)
+                    terms.append(term)
+                if t == 3:
+                    whole = keep.tile([P, J], F32, name="whole%d" % z)
+                    for part in (halves if z else [slice(0, J)]):
+                        nc.vector.tensor_tensor(whole[:, part], terms[0][:, part], terms[1][:, part], ADD if z else SUB)
+                        finish(z, t, whole[:, part], part)
+                    continue
+                turned = psum.tile([P, J], F32, name="turned", tag="turned%d" % ((z + t) % 2))
+                for i, term in enumerate(terms):
+                    for h in range(2):
+                        nc.tensor.matmul(
+                            turned[:, halves[h]], term[:, halves[h]], ident[:],
+                            start=(i, h) == (0, 0), stop=(i, h) == (1, 1), is_transpose=True,
+                        )
+                middle = keep.tile([P, J], F32, name="middle", tag="term_bn" if z else "middle")
+                nc.scalar.copy(middle[:], turned[:])
+                back = psum.tile([P, J], F32, name="back", tag="back%d" % z)
+                for h in range(2):
+                    nc.tensor.transpose(back[:, halves[h]], middle[:, halves[h]], ident[:])
+                backs.append(back)
+            if t + 1 < PACK:
+                gather_and_widen(t + 1)
+            for z, back in enumerate(backs):
+                finish(z, t, back[:])
 
         z_codes = [keep.tile([P, J], U32, name="z_codes%d" % z, align_bytes=64) for z in range(2)]
         z_plane = [keep.tile([P, J], U8, name="z_plane%d" % z, align_bytes=64) for z in range(2)]
-        acc = [psum.tile([P, J], F32, name="acc%d" % m) for m in range(2)]
-        for z, w_dtype in ((0, E5M2X4), (1, E4M3X4)):
-            nc.vector.quantize_mx(out=z_codes[z][:].bitcast(E4M3X4), scales=z_plane[z][:], in_=rounded[z][:])
+        acc = {(m, h): psum.tile([P, P], F32, name="acc%d%d" % (m, h)) for m in range(2) for h in range(2)}
+
+        def quantise(z, part):
+            nc.vector.quantize_mx(
+                out=z_codes[z][:, part].bitcast(E4M3X4),
+                scales=z_plane[z][:, part],
+                in_=rounded[z][:, part.start * PACK : part.stop * PACK],
+            )
+
+        def multiply(z, h):
             for m in range(2):
                 nc.tensor.matmul_mx(
-                    out=acc[m][:],
-                    lhsT=w_codes[z][:, m * P : (m + 1) * P].bitcast(w_dtype),
+                    out=acc[m, h][:],
+                    lhsT=w_codes[z][:, halves[m]].bitcast(E4M3X4 if z else E5M2X4),
                     lhsT_scale=w_plane[:, z * N + m * P : z * N + (m + 1) * P],
-                    rhs=z_codes[z][:].bitcast(E4M3X4),
-                    rhs_scale=z_plane[z][:],
+                    rhs=z_codes[z][:, halves[h]].bitcast(E4M3X4),
+                    rhs_scale=z_plane[z][:, halves[h]],
                     start=(z == 0),
                     stop=(z == 1),
                 )
-        result = [keep.tile([P, J], F32, name="result%d" % m) for m in range(2)]
-        nc.scalar.copy(result[0][:], acc[0][:])
-        nc.scalar.dma_start(out[0:P, :], result[0][:])
-        nc.vector.tensor_copy(result[1][:], acc[1][:])
-        nc.sync.dma_start(out[P : 2 * P, :], result[1][:])
+
+        quantise(0, slice(0, J))
+        for h in range(2):
+            multiply(0, h)
+        for h in range(2):
+            quantise(1, halves[h])
+            multiply(1, h)
+        for h in range(2):
+            result = [keep.tile([P, P], F32, name="result%d%d" % (m, h)) for m in range(2)]
+            nc.scalar.copy(result[0][:], acc[0, h][:])
+            nc.scalar.dma_start(out[halves[0], halves[h]], result[0][:])
+            nc.vector.tensor_copy(result[1][:], acc[1, h][:])
+            nc.sync.dma_start(out[halves[1], halves[h]], result[1][:])

@@ -88,22 +88,16 @@ def tile_list_turnedpairs_kernel(tc, ca, cb, cd, ce, sa, sb, w_words, w_scales, 
             nc.scalar.activation(rounded[z][:, part.start * PACK + t : part.stop * PACK : PACK], whole, COPY, scale=steps[z][:, t : t + 1])
 
         gather_and_widen(0)
-        for t in range(PACK):
+        for t in range(PACK - 1):
             gather(picked["a"], "a", t)
             gather(picked["b"], "b", t)
             backs = []
-            for z, pairs in enumerate((("ad", "bn" if t < 3 else "be"), ("ae", "bd"))):
+            for z, pairs in enumerate((("ad", "bn"), ("ae", "bd"))):
                 terms = []
                 for x, y in pairs:
                     term = keep.tile([P, J], F32, name="term", tag="term_" + x + y)
                     nc.vector.tensor_tensor(term[:], picked[x][:].bitcast(FP8), wide[y][:, cols(t)], MULT)
                     terms.append(term)
-                if t == 3:
-                    whole = keep.tile([P, J], F32, name="whole%d" % z)
-                    for part in (halves if z else [slice(0, J)]):
-                        nc.vector.tensor_tensor(whole[:, part], terms[0][:, part], terms[1][:, part], ADD if z else SUB)
-                        finish(z, t, whole[:, part], part)
-                    continue
                 turned = psum.tile([P, J], F32, name="turned", tag="turned%d" % ((z + t) % 2))
                 for i, term in enumerate(terms):
                     for h in range(2):
@@ -117,10 +111,22 @@ def tile_list_turnedpairs_kernel(tc, ca, cb, cd, ce, sa, sb, w_words, w_scales, 
                 for h in range(2):
                     nc.tensor.transpose(back[:, halves[h]], middle[:, halves[h]], ident[:])
                 backs.append(back)
-            if t + 1 < PACK:
-                gather_and_widen(t + 1)
+            gather_and_widen(t + 1)
             for z, back in enumerate(backs):
                 finish(z, t, back[:])
+
+        t = PACK - 1
+        gather(picked["a"], "a", t)
+        gather(picked["b"], "b", t)
+        for z, pairs in enumerate((("ad", "be"), ("ae", "bd"))):
+            terms = [keep.tile([P, J], F32, name="last_" + xy) for xy in pairs]
+            whole = keep.tile([P, J], F32, name="whole%d" % z)
+            for part in halves:
+                for term, (x, y) in zip(terms, pairs):
+                    nc.vector.tensor_tensor(term[:, part], picked[x][:, part].bitcast(FP8), wide[y][:, cols(t)][:, part], MULT)
+            for part in halves:
+                nc.vector.tensor_tensor(whole[:, part], terms[0][:, part], terms[1][:, part], ADD if z else SUB)
+                finish(z, t, whole[:, part], part)
 
         z_codes = [keep.tile([P, J], U32, name="z_codes%d" % z, align_bytes=64) for z in range(2)]
         z_plane = [keep.tile([P, J], U8, name="z_plane%d" % z, align_bytes=64) for z in range(2)]
@@ -145,15 +151,16 @@ def tile_list_turnedpairs_kernel(tc, ca, cb, cd, ce, sa, sb, w_words, w_scales, 
                     stop=(z == 1),
                 )
 
-        quantise(0, slice(0, J))
-        for h in range(2):
-            multiply(0, h)
-        for h in range(2):
-            quantise(1, halves[h])
-            multiply(1, h)
-        for h in range(2):
-            result = [keep.tile([P, P], F32, name="result%d%d" % (m, h)) for m in range(2)]
-            nc.scalar.copy(result[0][:], acc[0, h][:])
-            nc.scalar.dma_start(out[halves[0], halves[h]], result[0][:])
-            nc.vector.tensor_copy(result[1][:], acc[1, h][:])
-            nc.sync.dma_start(out[halves[1], halves[h]], result[1][:])
+        for z in range(2):
+            for h in range(2):
+                quantise(z, halves[h])
+                multiply(z, h)
+        first = keep.tile([P, 2, P], F32, name="first")
+        for m in range(2):
+            nc.scalar.copy(first[:, m, :], acc[m, 0][:])
+        nc.sync.dma_start(out.rearrange("(m p) j -> p m j", m=2)[:, :, halves[0]], first[:])
+        second = [keep.tile([P, P], F32, name="second%d" % m) for m in range(2)]
+        nc.vector.tensor_copy(second[0][:], acc[0, 1][:])
+        nc.sync.dma_start(out[halves[0], halves[1]], second[0][:])
+        nc.scalar.copy(second[1][:], acc[1, 1][:])
+        nc.scalar.dma_start(out[halves[1], halves[1]], second[1][:])

@@ -21,7 +21,11 @@ SUB = mybir.AluOpType.subtract
 COPY = mybir.ActivationFunctionType.Copy
 
 P = 128
-PACK = 4
+PLANES = 4
+LAST = PLANES - 1
+QUADRANT = 32
+HALVES = (slice(0, P), slice(P, 2 * P))
+ALL_J = slice(0, J)
 
 
 def tile_list_turnedpairs_kernel(tc, ca, cb, cd, ce, sa, sb, w_words, w_scales, w2_words, w2_scales, offs, offs2, out):
@@ -32,135 +36,132 @@ def tile_list_turnedpairs_kernel(tc, ca, cb, cd, ce, sa, sb, w_words, w_scales, 
 
         list1 = keep.tile([P, J // 16], U16, name="list1")
         list2 = keep.tile([P, J // 16], U16, name="list2")
-
         sources = {"d": (cd, list2), "e": (ce, list2), "a": (ca, list1), "b": (cb, list1)}
-        order = [(x, t) for t in range(PACK) for x in "deab"]
+
         tables = {}
         steps = {}
-        for x, t in order:
-            tables[x, t] = keep.tile([P, V], U8, name="table_%s%d" % (x, t))
-            nc.sync.dma_start(tables[x, t][:], sources[x][0].rearrange("(p t) v -> t p v", t=PACK)[t])
-            if (x, t) == ("d", 0):
-                nc.sync.dma_start(list2[:], offs2)
-            if (x, t) == ("e", 0):
-                nc.sync.dma_start(list1[:], offs)
-            if (x, t) == ("b", 0):
-                for z, src in ((0, sa), (1, sb)):
-                    steps[z] = keep.tile([P, PACK], F32, name="step%d" % z)
-                    nc.sync.dma_start(steps[z][:], src.rearrange("(p t) o -> p (t o)", t=PACK))
+        for t in range(PLANES):
+            for x in sources:
+                tables[x, t] = keep.tile([P, V], U8, name="table_%s%d" % (x, t))
+                nc.sync.dma_start(tables[x, t][:], sources[x][0].rearrange("(p t) v -> t p v", t=PLANES)[t])
+                if (x, t) == ("d", 0):
+                    nc.sync.dma_start(list2[:], offs2)
+                if (x, t) == ("e", 0):
+                    nc.sync.dma_start(list1[:], offs)
+            if t == 0:
+                for z, step in enumerate((sa, sb)):
+                    steps[z] = keep.tile([P, PLANES], F32, name="step%d" % z)
+                    nc.sync.dma_start(steps[z][:], step.rearrange("(p t) o -> p (t o)", t=PLANES))
 
         w_codes = {}
-        w_plane = keep.tile([P, 2 * N], U8, name="w_plane", align_bytes=64)
-        nc.gpsimd.memset(w_plane[:].bitcast(U32), 0)
-        for z, words in ((0, w_words), (1, w2_words)):
+        w_scale = keep.tile([P, 2 * N], U8, name="w_scale", align_bytes=64)
+        nc.gpsimd.memset(w_scale[:].bitcast(U32), 0)
+        for z, words in enumerate((w_words, w2_words)):
             w_codes[z] = keep.tile([P, N], U32, name="w_codes%d" % z, align_bytes=64)
             nc.sync.dma_start(w_codes[z][:].bitcast(I32), words[0].rearrange("p n r -> p (n r)").bitcast(I32))
-        for z, scales in ((0, w_scales), (1, w2_scales)):
-            for q in range(4):
+        for z, scales in enumerate((w_scales, w2_scales)):
+            for q in range(P // QUADRANT):
                 nc.sync.dma_start(
-                    w_plane[32 * q : 32 * q + 4, z * N : (z + 1) * N].bitcast(I32),
+                    w_scale[QUADRANT * q : QUADRANT * q + 4, z * N : (z + 1) * N].bitcast(I32),
                     scales[0][4 * q : 4 * q + 4, :].bitcast(I32),
                 )
 
         ident = keep.tile([P, P], F32, name="ident")
         make_identity(nc, ident[:])
+
         picked = {x: keep.tile([P, J], U8, name="picked_" + x) for x in "ab"}
-        wide = {y: keep.tile([P, PACK * J], F32, name="wide_" + y) for y in "den"}
-        rounded = [keep.tile([P, J * PACK], BF16, name="rounded%d" % z, align_bytes=64) for z in range(2)]
-        halves = [slice(0, P), slice(P, J)]
+        wide = {y: keep.tile([P, PLANES * J], F32, name="wide_" + y) for y in "den"}
+        rounded = [keep.tile([P, J * PLANES], BF16, name="rounded%d" % z, align_bytes=64) for z in range(2)]
 
         def cols(t):
             return slice(t * J, (t + 1) * J)
 
-        def gather(into, x, t):
+        def look_up(into, x, t):
             nc.vector.tensor_copy(into[:], tables[x, t][:].indirect(sources[x][1][:]))
 
-        def gather_and_widen(t):
+        def look_up_and_widen(t):
             for y in "de":
-                tag = "term_a" + y
-                codes = keep.tile([P, J], U8, name="second", tag=tag)
-                gather(codes, y, t)
+                codes = keep.tile([P, J], U8, name="codes", tag="term_a" + y)
+                look_up(codes, y, t)
                 nc.scalar.activation(wide[y][:, cols(t)], codes[:].bitcast(FP8), COPY)
-                if y == "e" and t < 3:
+                if y == "e" and t < LAST:
                     nc.scalar.activation(wide["n"][:, cols(t)], codes[:].bitcast(FP8), COPY, scale=-1.0)
 
-        def finish(z, t, whole, part=slice(0, J)):
-            nc.scalar.activation(rounded[z][:, part.start * PACK + t : part.stop * PACK : PACK], whole, COPY, scale=steps[z][:, t : t + 1])
+        def scale_and_round(z, t, total, part):
+            places = slice(part.start * PLANES + t, part.stop * PLANES, PLANES)
+            nc.scalar.activation(rounded[z][:, places], total, COPY, scale=steps[z][:, t : t + 1])
 
-        gather_and_widen(0)
-        for t in range(PACK - 1):
-            gather(picked["a"], "a", t)
-            gather(picked["b"], "b", t)
-            backs = []
+        look_up_and_widen(0)
+        for t in range(LAST):
+            look_up(picked["a"], "a", t)
+            look_up(picked["b"], "b", t)
+            sums = []
             for z, pairs in enumerate((("ad", "bn"), ("ae", "bd"))):
                 terms = []
                 for x, y in pairs:
-                    term = keep.tile([P, J], F32, name="term", tag="term_" + x + y)
+                    term = keep.tile([P, J], F32, name="term", tag="term_" + x + y + ("" if x == "a" else str(t)))
                     nc.vector.tensor_tensor(term[:], picked[x][:].bitcast(FP8), wide[y][:, cols(t)], MULT)
                     terms.append(term)
                 turned = psum.tile([P, J], F32, name="turned", tag="turned%d" % ((z + t) % 2))
                 for i, term in enumerate(terms):
-                    for h in range(2):
+                    for h, half in enumerate(HALVES):
                         nc.tensor.matmul(
-                            turned[:, halves[h]], term[:, halves[h]], ident[:],
-                            start=(i, h) == (0, 0), stop=(i, h) == (1, 1), is_transpose=True,
+                            turned[:, half],
+                            term[:, half],
+                            ident[:],
+                            start=(i, h) == (0, 0),
+                            stop=(i, h) == (1, 1),
+                            is_transpose=True,
                         )
-                middle = keep.tile([P, J], F32, name="middle", tag="term_bn" if z else "middle")
+                middle = keep.tile([P, J], F32, name="middle", tag="middle%d%d" % (z, t))
                 nc.scalar.copy(middle[:], turned[:])
                 back = psum.tile([P, J], F32, name="back", tag="back%d" % z)
-                for h in range(2):
-                    nc.tensor.transpose(back[:, halves[h]], middle[:, halves[h]], ident[:])
-                backs.append(back)
-            gather_and_widen(t + 1)
-            for z, back in enumerate(backs):
-                finish(z, t, back[:])
+                for half in HALVES:
+                    nc.tensor.transpose(back[:, half], middle[:, half], ident[:])
+                sums.append(back)
+            look_up_and_widen(t + 1)
+            for z, back in enumerate(sums):
+                scale_and_round(z, t, back[:], ALL_J)
 
-        t = PACK - 1
-        gather(picked["a"], "a", t)
-        gather(picked["b"], "b", t)
-        for z, pairs in enumerate((("ad", "be"), ("ae", "bd"))):
+        look_up(picked["a"], "a", LAST)
+        look_up(picked["b"], "b", LAST)
+        for z, (pairs, join) in enumerate(((("ad", "be"), SUB), (("ae", "bd"), ADD))):
             terms = [keep.tile([P, J], F32, name="last_" + xy) for xy in pairs]
-            whole = keep.tile([P, J], F32, name="whole%d" % z)
-            for part in halves:
+            total = keep.tile([P, J], F32, name="total%d" % z)
+            for half in HALVES:
                 for term, (x, y) in zip(terms, pairs):
-                    nc.vector.tensor_tensor(term[:, part], picked[x][:, part].bitcast(FP8), wide[y][:, cols(t)][:, part], MULT)
-            for part in halves:
-                nc.vector.tensor_tensor(whole[:, part], terms[0][:, part], terms[1][:, part], ADD if z else SUB)
-                finish(z, t, whole[:, part], part)
+                    nc.vector.tensor_tensor(term[:, half], picked[x][:, half].bitcast(FP8), wide[y][:, cols(LAST)][:, half], MULT)
+            for half in HALVES:
+                nc.vector.tensor_tensor(total[:, half], terms[0][:, half], terms[1][:, half], join)
+                scale_and_round(z, LAST, total[:, half], half)
 
         z_codes = [keep.tile([P, J], U32, name="z_codes%d" % z, align_bytes=64) for z in range(2)]
-        z_plane = [keep.tile([P, J], U8, name="z_plane%d" % z, align_bytes=64) for z in range(2)]
+        z_scale = [keep.tile([P, J], U8, name="z_scale%d" % z, align_bytes=64) for z in range(2)]
         acc = {(m, h): psum.tile([P, P], F32, name="acc%d%d" % (m, h)) for m in range(2) for h in range(2)}
-
-        def quantise(z, part):
-            nc.vector.quantize_mx(
-                out=z_codes[z][:, part].bitcast(E4M3X4),
-                scales=z_plane[z][:, part],
-                in_=rounded[z][:, part.start * PACK : part.stop * PACK],
-            )
-
-        def multiply(z, h):
-            for m in range(2):
-                nc.tensor.matmul_mx(
-                    out=acc[m, h][:],
-                    lhsT=w_codes[z][:, halves[m]].bitcast(E4M3X4 if z else E5M2X4),
-                    lhsT_scale=w_plane[:, z * N + m * P : z * N + (m + 1) * P],
-                    rhs=z_codes[z][:, halves[h]].bitcast(E4M3X4),
-                    rhs_scale=z_plane[z][:, halves[h]],
-                    start=(z == 0),
-                    stop=(z == 1),
+        for z, w_dtype in enumerate((E5M2X4, E4M3X4)):
+            for h, half in enumerate(HALVES):
+                nc.vector.quantize_mx(
+                    out=z_codes[z][:, half].bitcast(E4M3X4),
+                    scales=z_scale[z][:, half],
+                    in_=rounded[z][:, half.start * PLANES : half.stop * PLANES],
                 )
+                for m in range(2):
+                    nc.tensor.matmul_mx(
+                        out=acc[m, h][:],
+                        lhsT=w_codes[z][:, HALVES[m]].bitcast(w_dtype),
+                        lhsT_scale=w_scale[:, z * N + m * P : z * N + (m + 1) * P],
+                        rhs=z_codes[z][:, half].bitcast(E4M3X4),
+                        rhs_scale=z_scale[z][:, half],
+                        start=(z == 0),
+                        stop=(z == 1),
+                    )
 
-        for z in range(2):
-            for h in range(2):
-                quantise(z, halves[h])
-                multiply(z, h)
         first = keep.tile([P, 2, P], F32, name="first")
         for m in range(2):
             nc.scalar.copy(first[:, m, :], acc[m, 0][:])
-        nc.sync.dma_start(out.rearrange("(m p) j -> p m j", m=2)[:, :, halves[0]], first[:])
+        nc.sync.dma_start(out.rearrange("(m p) j -> p m j", m=2)[:, :, HALVES[0]], first[:])
         second = [keep.tile([P, P], F32, name="second%d" % m) for m in range(2)]
         nc.vector.tensor_copy(second[0][:], acc[0, 1][:])
-        nc.sync.dma_start(out[halves[0], halves[1]], second[0][:])
+        nc.sync.dma_start(out[HALVES[0], HALVES[1]], second[0][:])
         nc.scalar.copy(second[1][:], acc[1, 1][:])
-        nc.scalar.dma_start(out[halves[1], halves[1]], second[1][:])
+        nc.scalar.dma_start(out[HALVES[1], HALVES[1]], second[1][:])

from contextlib import ExitStack

import concourse.mybir as mybir
from concourse.masks import make_identity

K, V, J, N = 512, 512, 256, 256
FLOPS = 2 * 2 * K * N * J

F32 = mybir.dt.float32
BF16 = mybir.dt.bfloat16
I32 = mybir.dt.int32
U32 = mybir.dt.uint32
U16 = mybir.dt.uint16
U8 = mybir.dt.uint8
FP8 = mybir.dt.float8_e4m3fn
E4M3X4 = mybir.dt.float8_e4m3fn_x4
E5M2X4 = mybir.dt.float8_e5m2_x4
MULT = mybir.AluOpType.mult
ADD = mybir.AluOpType.add
SUB = mybir.AluOpType.subtract
COPY = mybir.ActivationFunctionType.Copy

P = 128
PLANES = 4
LAST = PLANES - 1
QUADRANT = 32
HALVES = (slice(0, P), slice(P, 2 * P))
ALL_J = slice(0, J)


def tile_list_turnedpairs_kernel(tc, ca, cb, cd, ce, sa, sb, w_words, w_scales, w2_words, w2_scales, offs, offs2, out):
    nc = tc.nc
    with ExitStack() as ctx:
        keep = ctx.enter_context(tc.tile_pool(name="keep", bufs=1))
        psum = ctx.enter_context(tc.psum_pool(name="psum", bufs=1))

        list1 = keep.tile([P, J // 16], U16, name="list1")
        list2 = keep.tile([P, J // 16], U16, name="list2")
        sources = {"d": (cd, list2), "e": (ce, list2), "a": (ca, list1), "b": (cb, list1)}

        tables = {}
        steps = {}
        for t in range(PLANES):
            for x in sources:
                tables[x, t] = keep.tile([P, V], U8, name="table_%s%d" % (x, t))
                nc.sync.dma_start(tables[x, t][:], sources[x][0].rearrange("(p t) v -> t p v", t=PLANES)[t])
                if (x, t) == ("d", 0):
                    nc.sync.dma_start(list2[:], offs2)
                if (x, t) == ("e", 0):
                    nc.sync.dma_start(list1[:], offs)
            if t == 0:
                for z, step in enumerate((sa, sb)):
                    steps[z] = keep.tile([P, PLANES], F32, name="step%d" % z)
                    nc.sync.dma_start(steps[z][:], step.rearrange("(p t) o -> p (t o)", t=PLANES))

        w_codes = {}
        w_scale = keep.tile([P, 2 * N], U8, name="w_scale", align_bytes=64)
        nc.gpsimd.memset(w_scale[:].bitcast(U32), 0)
        for z, words in enumerate((w_words, w2_words)):
            w_codes[z] = keep.tile([P, N], U32, name="w_codes%d" % z, align_bytes=64)
            nc.sync.dma_start(w_codes[z][:].bitcast(I32), words[0].rearrange("p n r -> p (n r)").bitcast(I32))
        for z, scales in enumerate((w_scales, w2_scales)):
            for q in range(P // QUADRANT):
                nc.sync.dma_start(
                    w_scale[QUADRANT * q : QUADRANT * q + 4, z * N : (z + 1) * N].bitcast(I32),
                    scales[0][4 * q : 4 * q + 4, :].bitcast(I32),
                )

        ident = keep.tile([P, P], F32, name="ident")
        make_identity(nc, ident[:])

        picked = {x: keep.tile([P, J], U8, name="picked_" + x) for x in "ab"}
        wide = {y: keep.tile([P, PLANES * J], F32, name="wide_" + y) for y in "den"}
        rounded = [keep.tile([P, J * PLANES], BF16, name="rounded%d" % z, align_bytes=64) for z in range(2)]

        def cols(t):
            return slice(t * J, (t + 1) * J)

        def look_up(into, x, t):
            nc.vector.tensor_copy(into[:], tables[x, t][:].indirect(sources[x][1][:]))

        def look_up_and_widen(t):
            for y in "de":
                codes = keep.tile([P, J], U8, name="codes", tag="term_a" + y)
                look_up(codes, y, t)
                nc.scalar.activation(wide[y][:, cols(t)], codes[:].bitcast(FP8), COPY)
                if y == "e" and t < LAST:
                    nc.scalar.activation(wide["n"][:, cols(t)], codes[:].bitcast(FP8), COPY, scale=-1.0)

        def scale_and_round(z, t, total, part):
            places = slice(part.start * PLANES + t, part.stop * PLANES, PLANES)
            nc.scalar.activation(rounded[z][:, places], total, COPY, scale=steps[z][:, t : t + 1])

        look_up_and_widen(0)
        for t in range(LAST):
            look_up(picked["a"], "a", t)
            look_up(picked["b"], "b", t)
            sums = []
            for z, pairs in enumerate((("ad", "bn"), ("ae", "bd"))):
                terms = []
                for x, y in pairs:
                    term = keep.tile([P, J], F32, name="term", tag="term_" + x + y + ("" if x == "a" else str(t)))
                    nc.vector.tensor_tensor(term[:], picked[x][:].bitcast(FP8), wide[y][:, cols(t)], MULT)
                    terms.append(term)
                turned = psum.tile([P, J], F32, name="turned", tag="turned%d" % ((z + t) % 2))
                for i, term in enumerate(terms):
                    for h, half in enumerate(HALVES):
                        nc.tensor.matmul(
                            turned[:, half],
                            term[:, half],
                            ident[:],
                            start=(i, h) == (0, 0),
                            stop=(i, h) == (1, 1),
                            is_transpose=True,
                        )
                middle = keep.tile([P, J], F32, name="middle", tag="middle%d%d" % (z, t))
                nc.scalar.copy(middle[:], turned[:])
                back = psum.tile([P, J], F32, name="back", tag="back%d" % z)
                for half in HALVES:
                    nc.tensor.transpose(back[:, half], middle[:, half], ident[:])
                sums.append(back)
            look_up_and_widen(t + 1)
            for z, back in enumerate(sums):
                scale_and_round(z, t, back[:], ALL_J)

        look_up(picked["a"], "a", LAST)
        look_up(picked["b"], "b", LAST)
        for z, (pairs, join) in enumerate(((("ad", "be"), SUB), (("ae", "bd"), ADD))):
            terms = [keep.tile([P, J], F32, name="last_" + xy) for xy in pairs]
            total = keep.tile([P, J], F32, name="total%d" % z)
            for half in HALVES:
                for term, (x, y) in zip(terms, pairs):
                    nc.vector.tensor_tensor(term[:, half], picked[x][:, half].bitcast(FP8), wide[y][:, cols(LAST)][:, half], MULT)
            for half in HALVES:
                nc.vector.tensor_tensor(total[:, half], terms[0][:, half], terms[1][:, half], join)
                scale_and_round(z, LAST, total[:, half], half)

        z_codes = [keep.tile([P, J], U32, name="z_codes%d" % z, align_bytes=64) for z in range(2)]
        z_scale = [keep.tile([P, J], U8, name="z_scale%d" % z, align_bytes=64) for z in range(2)]
        acc = {(m, h): psum.tile([P, P], F32, name="acc%d%d" % (m, h)) for m in range(2) for h in range(2)}
        for z, w_dtype in enumerate((E5M2X4, E4M3X4)):
            for h, half in enumerate(HALVES):
                nc.vector.quantize_mx(
                    out=z_codes[z][:, half].bitcast(E4M3X4),
                    scales=z_scale[z][:, half],
                    in_=rounded[z][:, half.start * PLANES : half.stop * PLANES],
                )
                for m in range(2):
                    nc.tensor.matmul_mx(
                        out=acc[m, h][:],
                        lhsT=w_codes[z][:, HALVES[m]].bitcast(w_dtype),
                        lhsT_scale=w_scale[:, z * N + m * P : z * N + (m + 1) * P],
                        rhs=z_codes[z][:, half].bitcast(E4M3X4),
                        rhs_scale=z_scale[z][:, half],
                        start=(z == 0),
                        stop=(z == 1),
                    )

        first = keep.tile([P, 2, P], F32, name="first")
        for m in range(2):
            nc.scalar.copy(first[:, m, :], acc[m, 0][:])
        nc.sync.dma_start(out.rearrange("(m p) j -> p m j", m=2)[:, :, HALVES[0]], first[:])
        second = [keep.tile([P, P], F32, name="second%d" % m) for m in range(2)]
        nc.vector.tensor_copy(second[0][:], acc[0, 1][:])
        nc.sync.dma_start(out[HALVES[0], HALVES[1]], second[0][:])
        nc.scalar.copy(second[1][:], acc[1, 1][:])
        nc.scalar.dma_start(out[HALVES[1], HALVES[1]], second[1][:])
